import numpy as np
import ml_dtypes


def mxq(x, axis, fmt="e4m3"):
    dtype, down = {"e4m3": (ml_dtypes.float8_e4m3fn, 7), "e5m2": (ml_dtypes.float8_e5m2, 14)}[fmt]
    v = np.moveaxis(np.asarray(x, np.float32).astype(ml_dtypes.bfloat16).astype(np.float64), axis, -1)
    blocks = v.reshape(v.shape[:-1] + (-1, 32))
    amax = np.abs(blocks).max(-1, keepdims=True)
    byte = np.maximum(np.where(amax > 0, np.frexp(amax)[1] - 1 + 127, 0) - down, 1)
    scale = np.exp2(byte - 127.0)
    codes = (blocks / scale).astype(np.float32).astype(dtype).astype(np.float64)
    return np.moveaxis((codes * scale).reshape(v.shape), -1, axis)


WIDE = False


def mx_kscale(k):
    if not WIDE:
        return np.ones(k)
    levels = np.array([10, -10, 5, -5, 0])
    if k % 512:
        return np.exp2(np.random.permutation(np.resize(levels, k // 32))).repeat(32)
    a = np.empty((k // 512, 16))
    for p in range(k // 512):
        a[p, :8] = np.random.permutation(np.resize(levels, 8))
        for g in range(8):
            far = levels[np.abs(levels - a[p, g]) >= 10]
            a[p, g + 8] = far[np.random.randint(len(far))]
    return np.exp2(a.ravel()).repeat(32)


def f64(x):
    return np.asarray(x).astype(np.float64)


def striped(idx):
    return np.tile(np.asarray(idx).reshape(-1, 16).T, (8, 1)).astype(np.uint16)


def unstriped(offs):
    return offs[:16].T.reshape(-1).astype(np.int64)


E2M1 = np.array([0.0, 0.5, 1.0, 1.5, 2.0, 3.0, 4.0, 6.0, -0.0, -0.5, -1.0, -1.5, -2.0, -3.0, -4.0, -6.0])


def pack_weight(w, fmt):
    k, n = w.shape
    w = f64(np.asarray(w, np.float32).astype(ml_dtypes.bfloat16)).reshape(k // 32, 32, n)
    amax = np.abs(w).max(1)
    if fmt == "e4m3":
        byte = np.frexp(amax)[1] - 1 + 127 - 7
    else:
        mant, ex = np.frexp(amax / 6.0)
        byte = np.where(mant > 0.5, ex, ex - 1) + 127
    byte = np.clip(np.where(amax > 0, byte, 1), 1, 254)
    scaled = (w * np.exp2(127.0 - byte)[:, None, :]).reshape(k, n).astype(np.float32)
    by_word = np.ascontiguousarray(scaled.reshape(k // 512, 128, 4, n).transpose(0, 1, 3, 2))
    if fmt == "e4m3":
        words = by_word.astype(ml_dtypes.float8_e4m3fn).view(np.uint8)
    else:
        c = by_word.astype(ml_dtypes.float4_e2m1fn).view(np.uint8) & 0xF
        words = (c[..., 0::2] | (c[..., 1::2] << 4)).reshape(k // 512, 128, 2 * n)
    return np.ascontiguousarray(words), np.ascontiguousarray(byte.astype(np.uint8).reshape(k // 512, 16, n))


def unpack_weight(words, scales, fmt):
    g, _, n = scales.shape
    words = np.ascontiguousarray(words).reshape(g, 128, n, -1)
    if fmt == "e4m3":
        vals = words.view(ml_dtypes.float8_e4m3fn).astype(np.float64)
    else:
        nib = np.empty((g, 128, n, 4), np.uint8)
        nib[..., 0::2] = words & 0xF
        nib[..., 1::2] = words >> 4
        vals = E2M1[nib]
    vals = vals * np.repeat(np.exp2(scales.astype(np.float64) - 127.0), 8, axis=1)[..., None]
    return vals.transpose(0, 1, 3, 2).reshape(g * 512, n)


def softplus(v):
    return np.log(1.0 + np.exp(v))


K, T, J, B, L, N = 1024, 2048, 512, 128, 512, 512


def setup_inputs():
    n = np.random.standard_normal
    idx = np.random.permutation(T)[:J]
    fk = mx_kscale(K)
    fl = mx_kscale(L)
    xqp = pack_weight(n((K, T)) / fk[:, None], "e4m3")
    cxp = pack_weight(n((L, B)) / fl[:, None], "e2m1")
    wcp = pack_weight(n((L, N)) * 1 / np.sqrt(L) * fl[:, None], "e4m3")
    return {
        "xq_words": xqp[0],
        "xq_scales": xqp[1],
        "wa": (n((K, N)) * 1 / np.sqrt(K) * fk[:, None]).astype(np.float32),
        "ga": (np.random.uniform(0.4, 1.2, (1, J))).astype(np.float32),
        "cx_words": cxp[0],
        "cx_scales": cxp[1],
        "wc_words": wcp[0],
        "wc_scales": wcp[1],
        "offs": striped(idx),
    }


def reference(xq_words, xq_scales, wa, ga, cx_words, cx_scales, wc_words, wc_scales, offs):
    idx = unstriped(offs)
    xqu = unpack_weight(xq_words, xq_scales, "e4m3")
    cxu = unpack_weight(cx_words, cx_scales, "e2m1")
    wcu = unpack_weight(wc_words, wc_scales, "e4m3")
    waq = mxq(f64(wa), 0, "e4m3")
    xqidxg = xqu[:, idx]
    p = waq.T @ xqidxg
    w = softplus(p) * f64(ga)
    s = w.reshape(N, B, J // B).sum(axis=2)
    q = wcu.T @ cxu
    y = s + q
    return y

@@ -1,0 +1,184 @@
+import math
+from contextlib import ExitStack
+
+import concourse.mybir as mybir
+from concourse.masks import make_identity
+
+K, T, J, B, L, N = 1024, 2048, 512, 128, 512, 512
+FLOPS = 2 * K * N * J + 2 * L * N * B
+
+F32 = mybir.dt.float32
+BF16 = mybir.dt.bfloat16
+I32 = mybir.dt.int32
+U32 = mybir.dt.uint32
+U16 = mybir.dt.uint16
+U8 = mybir.dt.uint8
+FP8X4 = mybir.dt.float8_e4m3fn_x4
+FP4X4 = mybir.dt.float4_e2m1fn_x4
+ALU = mybir.AluOpType
+ACT = mybir.ActivationFunctionType
+
+P = 128
+PACK = 4
+K_PASS = P * PACK
+PASSES = K // K_PASS
+GROUP = J // B
+CHUNK = 128
+CHUNKS = N // CHUNK
+EXP_CAP = 2.0**32
+X_CAP = math.log(EXP_CAP)
+TABLE_PIECES = (4, 2)
+SCALAR_CASTS = ((0, 0), (0, 1), (1, 0), (2, 0))
+
+
+def load_scale_rows(queue, plane, scales, passes):
+    for quad in range(4):
+        queue.dma_start(
+            out=plane[32 * quad : 32 * quad + 4 * passes, :].bitcast(I32),
+            in_=scales[:, 4 * quad : 4 * quad + 4, :].bitcast(I32),
+        )
+
+
+def tile_list_expert_then_pool_kernel(tc, xq_words, xq_scales, wa, ga, cx_words, cx_scales, wc_words, wc_scales, offs, out):
+    nc = tc.nc
+    with ExitStack() as ctx:
+        sb = ctx.enter_context(tc.tile_pool(name="sb", bufs=1))
+        ps = ctx.enter_context(tc.psum_pool(name="ps", bufs=1))
+
+        offsets = sb.tile([P, J // 16], U16, name="offsets")
+        nc.sync.dma_start(offsets[:], offs)
+
+        x_plane = sb.tile([P, T], U8, name="x_plane", align_bytes=64)
+        nc.gpsimd.memset(x_plane[:].bitcast(I32), 0)
+        load_scale_rows(nc.sync, x_plane, xq_scales, PASSES)
+
+        gate = sb.tile([P, GROUP], F32, name="gate")
+        nc.sync.dma_start(out=gate[:], in_=ga.rearrange("o (b t) -> (o b) t", t=GROUP))
+        cx_codes = sb.tile([P, 2 * B], U8, name="cx_codes", align_bytes=64)
+        nc.sync.dma_start(out=cx_codes[:].bitcast(I32), in_=cx_words[0].bitcast(I32))
+
+        x_table = []
+        for a in range(PASSES):
+            table = sb.tile([P, T], U32, name=f"x_table{a}", align_bytes=64)
+            words = xq_words[a].rearrange("p n t -> p (n t)").bitcast(I32)
+            width = T // TABLE_PIECES[a]
+            for lo in range(0, T, width):
+                nc.sync.dma_start(out=table[:, lo : lo + width].bitcast(I32), in_=words[:, lo : lo + width])
+            x_table.append(table)
+
+        w_raw = {}
+        for c in range(CHUNKS):
+            for a in range(PASSES):
+                raw = sb.tile([P, PACK, CHUNK], F32, name=f"w_raw{c}_{a}")
+                rows = wa[a * K_PASS : (a + 1) * K_PASS, c * CHUNK : (c + 1) * CHUNK]
+                nc.sync.dma_start(out=raw[:], in_=rows.rearrange("(p j) n -> p j n", j=PACK))
+                w_raw[c, a] = raw
+
+        wc_codes = sb.tile([P, N], U32, name="wc_codes", align_bytes=64)
+        wc_plane = sb.tile([P, N], U8, name="wc_plane", align_bytes=64)
+        cx_plane = sb.tile([P, B], U8, name="cx_plane", align_bytes=64)
+        nc.vector.memset(wc_plane[:].bitcast(I32), 0)
+        nc.vector.memset(cx_plane[:].bitcast(I32), 0)
+        nc.sync.dma_start(out=wc_codes[:].bitcast(I32), in_=wc_words[0].rearrange("p n t -> p (n t)").bitcast(I32))
+        load_scale_rows(nc.sync, wc_plane, wc_scales, 1)
+        load_scale_rows(nc.sync, cx_plane, cx_scales, 1)
+
+        identity = sb.tile([P, P], F32, name="identity")
+        make_identity(nc, identity[:])
+
+        cap_terms = sb.tile([P, GROUP], F32, name="cap_terms")
+        cap_sum = sb.tile([P, 1], F32, name="cap_sum")
+        nc.scalar.activation(cap_terms[:], gate[:], ACT.Identity, scale=-X_CAP, accum_out=cap_sum[:])
+
+        picked_plane = sb.tile([P, J], U8, name="picked_plane", align_bytes=64)
+        x_scale = sb.tile([P, J], U8, name="x_scale", align_bytes=64)
+        nc.vector.tensor_copy(picked_plane[:], x_plane[:].indirect(offsets[:]))
+        nc.vector.tensor_copy(
+            x_scale[:].rearrange("p (t b) -> p t b", t=GROUP), picked_plane[:].rearrange("p (b t) -> p t b", t=GROUP)
+        )
+        x_codes = []
+        for a in range(PASSES):
+            picked = sb.tile([P, J], U32, name=f"picked{a}", align_bytes=64)
+            codes = sb.tile([P, J], U32, name=f"x_codes{a}", align_bytes=64)
+            nc.vector.tensor_copy(picked[:], x_table[a][:].indirect(offsets[:]))
+            nc.vector.tensor_copy(
+                codes[:].rearrange("p (t b) -> p t b", t=GROUP), picked[:].rearrange("p (b t) -> p t b", t=GROUP)
+            )
+            x_codes.append(codes)
+
+        expo = sb.tile([P, CHUNKS, GROUP * CHUNK], F32, name="expo")
+        p_banks = []
+        for c in range(CHUNKS):
+            p_bank = ps.tile([P, GROUP, CHUNK], F32, name=f"p_bank{c}", tag=f"p{c}")
+            for a in range(PASSES):
+                grouped = sb.tile([P, CHUNK * PACK], BF16, name=f"grouped{c}_{a}", align_bytes=64)
+                dst = grouped[:].rearrange("p (m i j) -> p m j i", i=4, j=PACK)
+                src = w_raw[c, a][:].rearrange("p j (m i) -> p m j i", i=4)
+                if (c, a) in SCALAR_CASTS:
+                    nc.scalar.copy(dst, src)
+                else:
+                    nc.vector.tensor_copy(dst, src)
+                w_codes = sb.tile([P, CHUNK], U32, name=f"w_codes{c}_{a}", align_bytes=64)
+                w_scale = sb.tile([P, CHUNK], U8, name=f"w_scale{c}_{a}", align_bytes=64)
+                nc.vector.quantize_mx(out=w_codes[:].bitcast(FP8X4), scales=w_scale[:], in_=grouped[:])
+                for t in range(GROUP):
+                    cols = slice(t * B, (t + 1) * B)
+                    nc.tensor.matmul_mx(
+                        out=p_bank[:, t, :],
+                        lhsT=x_codes[a][:, cols].bitcast(FP8X4),
+                        lhsT_scale=x_scale[4 * a : P, cols],
+                        rhs=w_codes[:].bitcast(FP8X4),
+                        rhs_scale=w_scale[:],
+                        start=(a == 0 and t == 0),
+                        stop=(a == PASSES - 1 and t == GROUP - 1),
+                    )
+            nc.scalar.activation(expo[:, c, :], p_bank[:].rearrange("p t n -> p (t n)"), ACT.Exp)
+            p_banks.append(p_bank)
+
+        one_plus = sb.tile([P, CHUNKS, GROUP * CHUNK], F32, name="one_plus")
+        nc.vector.tensor_scalar(one_plus[:], expo[:], EXP_CAP, 1.0, ALU.min, ALU.add)
+
+        linear = []
+        for c in range(CHUNKS):
+            lin = sb.tile([P, GROUP, CHUNK], F32, name=f"linear{c}")
+            nc.vector.scalar_tensor_tensor(
+                lin[:], p_banks[c][:], X_CAP, gate[:].unsqueeze(2).to_broadcast([P, GROUP, CHUNK]), ALU.max, ALU.mult
+            )
+            linear.append(lin)
+
+        q_bank = ps.tile([P, N], F32, name="q_bank", tag="p0")
+        nc.tensor.matmul_mx(
+            out=q_bank[:],
+            lhsT=cx_codes[:].bitcast(FP4X4),
+            lhsT_scale=cx_plane[:],
+            rhs=wc_codes[:].bitcast(FP8X4),
+            rhs_scale=wc_plane[:],
+            start=True,
+            stop=True,
+        )
+        context = sb.tile([P, N], F32, name="context")
+        nc.vector.tensor_scalar(context[:], q_bank[:], cap_sum[:], None, ALU.add)
+
+        o_banks = []
+        for c in range(CHUNKS):
+            o_bank = ps.tile([P, B], F32, name=f"o_bank{c}", tag=f"o{c}")
+            for t in range(GROUP):
+                nc.tensor.matmul(o_bank[:], linear[c][:, t, :], identity[:], start=(t == 0), stop=False, is_transpose=True)
+            o_banks.append(o_bank)
+        for c in range(CHUNKS):
+            nc.tensor.matmul(
+                o_banks[c][:], context[:, c * CHUNK : (c + 1) * CHUNK], identity[:], start=False, stop=False, is_transpose=True
+            )
+
+        for c in range(CHUNKS):
+            logs = sb.tile([P, GROUP, CHUNK], F32, name=f"logs{c}")
+            nc.scalar.activation(logs[:].rearrange("p t n -> p (t n)"), one_plus[:, c, :], ACT.Ln)
+            weighted = sb.tile([P, GROUP, CHUNK], F32, name=f"weighted{c}")
+            for t in range(GROUP):
+                nc.vector.tensor_scalar(weighted[:, t, :], logs[:, t, :], gate[:, t : t + 1], None, ALU.mult)
+                nc.tensor.matmul(
+                    o_banks[c][:], weighted[:, t, :], identity[:], start=False, stop=(t == GROUP - 1), is_transpose=True
+                )
+            result = sb.tile([P, B], F32, name=f"result{c}")
+            nc.vector.tensor_copy(result[:], o_banks[c][:])
+            nc.sync.dma_start(out=out[c * CHUNK : (c + 1) * CHUNK, :], in_=result[:])

@@ -27,8 +27,9 @@ CHUNK = 128
 CHUNKS = N // CHUNK
 EXP_CAP = 2.0**32
 X_CAP = math.log(EXP_CAP)
-TABLE_PIECES = (4, 2)
-SCALAR_CASTS = ((0, 0), (0, 1), (1, 0), (2, 0))
+W_LOADS = ((0, 0, 4), (1, 0, 1), (1, 1, 1), (1, 2, 1), (1, 3, 1))
+ORDER = tuple((c, a) for a in range(PASSES) for c in range(CHUNKS))
+SCALAR_CHUNKS = (3, 2)
 
 
 def load_scale_rows(queue, plane, scales, passes):
@@ -50,103 +51,131 @@ def tile_list_expert_then_pool_kernel(tc, xq_words, xq_scales, wa, ga, cx_words,
 
         x_plane = sb.tile([P, T], U8, name="x_plane", align_bytes=64)
         nc.gpsimd.memset(x_plane[:].bitcast(I32), 0)
+        x_table = [sb.tile([P, T], U32, name=f"x_table{a}", align_bytes=64) for a in range(PASSES)]
+        x_words = [xq_words[a].rearrange("p n t -> p (n t)").bitcast(I32) for a in range(PASSES)]
+        nc.sync.dma_start(out=x_table[0][:].bitcast(I32), in_=x_words[0])
         load_scale_rows(nc.sync, x_plane, xq_scales, PASSES)
-
         gate = sb.tile([P, GROUP], F32, name="gate")
         nc.sync.dma_start(out=gate[:], in_=ga.rearrange("o (b t) -> (o b) t", t=GROUP))
-        cx_codes = sb.tile([P, 2 * B], U8, name="cx_codes", align_bytes=64)
-        nc.sync.dma_start(out=cx_codes[:].bitcast(I32), in_=cx_words[0].bitcast(I32))
-
-        x_table = []
-        for a in range(PASSES):
-            table = sb.tile([P, T], U32, name=f"x_table{a}", align_bytes=64)
-            words = xq_words[a].rearrange("p n t -> p (n t)").bitcast(I32)
-            width = T // TABLE_PIECES[a]
-            for lo in range(0, T, width):
-                nc.sync.dma_start(out=table[:, lo : lo + width].bitcast(I32), in_=words[:, lo : lo + width])
-            x_table.append(table)
 
         w_raw = {}
-        for c in range(CHUNKS):
-            for a in range(PASSES):
-                raw = sb.tile([P, PACK, CHUNK], F32, name=f"w_raw{c}_{a}")
-                rows = wa[a * K_PASS : (a + 1) * K_PASS, c * CHUNK : (c + 1) * CHUNK]
-                nc.sync.dma_start(out=raw[:], in_=rows.rearrange("(p j) n -> p j n", j=PACK))
-                w_raw[c, a] = raw
+        for a, first, count in W_LOADS:
+            raw = sb.tile([P, PACK, count * CHUNK], F32, name=f"w_raw{a}_{first}")
+            rows = wa[a * K_PASS : (a + 1) * K_PASS, first * CHUNK : (first + count) * CHUNK]
+            nc.sync.dma_start(out=raw[:], in_=rows.rearrange("(p j) n -> p j n", j=PACK))
+            for c in range(count):
+                w_raw[first + c, a] = raw[:, :, c * CHUNK : (c + 1) * CHUNK]
+            if a == 0:
+                nc.sync.dma_start(out=x_table[1][:].bitcast(I32), in_=x_words[1])
 
         wc_codes = sb.tile([P, N], U32, name="wc_codes", align_bytes=64)
         wc_plane = sb.tile([P, N], U8, name="wc_plane", align_bytes=64)
+        cx_codes = sb.tile([P, 2 * B], U8, name="cx_codes", align_bytes=64)
         cx_plane = sb.tile([P, B], U8, name="cx_plane", align_bytes=64)
-        nc.vector.memset(wc_plane[:].bitcast(I32), 0)
-        nc.vector.memset(cx_plane[:].bitcast(I32), 0)
         nc.sync.dma_start(out=wc_codes[:].bitcast(I32), in_=wc_words[0].rearrange("p n t -> p (n t)").bitcast(I32))
-        load_scale_rows(nc.sync, wc_plane, wc_scales, 1)
-        load_scale_rows(nc.sync, cx_plane, cx_scales, 1)
-
+        nc.sync.dma_start(out=cx_codes[:].bitcast(I32), in_=cx_words[0].bitcast(I32))
         identity = sb.tile([P, P], F32, name="identity")
         make_identity(nc, identity[:])
+        nc.gpsimd.memset(wc_plane[:].bitcast(I32), 0)
+        nc.gpsimd.memset(cx_plane[:].bitcast(I32), 0)
+        load_scale_rows(nc.gpsimd, wc_plane, wc_scales, 1)
+        load_scale_rows(nc.sync, cx_plane, cx_scales, 1)
 
         cap_terms = sb.tile([P, GROUP], F32, name="cap_terms")
         cap_sum = sb.tile([P, 1], F32, name="cap_sum")
         nc.scalar.activation(cap_terms[:], gate[:], ACT.Identity, scale=-X_CAP, accum_out=cap_sum[:])
 
+        def gather_words(a):
+            codes = sb.tile([P, J], U32, name=f"x_codes{a}", align_bytes=64)
+            nc.vector.tensor_copy(codes[:].rearrange("p (t b) -> p b t", t=GROUP), x_table[a][:].indirect(offsets[:]))
+            return codes
+
+        x_codes = [gather_words(0)]
         picked_plane = sb.tile([P, J], U8, name="picked_plane", align_bytes=64)
-        x_scale = sb.tile([P, J], U8, name="x_scale", align_bytes=64)
         nc.vector.tensor_copy(picked_plane[:], x_plane[:].indirect(offsets[:]))
+        x_scale = sb.tile([P, J], U8, name="x_scale", align_bytes=64)
         nc.vector.tensor_copy(
             x_scale[:].rearrange("p (t b) -> p t b", t=GROUP), picked_plane[:].rearrange("p (b t) -> p t b", t=GROUP)
         )
-        x_codes = []
-        for a in range(PASSES):
-            picked = sb.tile([P, J], U32, name=f"picked{a}", align_bytes=64)
-            codes = sb.tile([P, J], U32, name=f"x_codes{a}", align_bytes=64)
-            nc.vector.tensor_copy(picked[:], x_table[a][:].indirect(offsets[:]))
-            nc.vector.tensor_copy(
-                codes[:].rearrange("p (t b) -> p t b", t=GROUP), picked[:].rearrange("p (b t) -> p t b", t=GROUP)
-            )
-            x_codes.append(codes)
 
+        linear = sb.tile([P, GROUP, CHUNKS, CHUNK], F32, name="linear", align_bytes=64)
         expo = sb.tile([P, CHUNKS, GROUP * CHUNK], F32, name="expo")
-        p_banks = []
-        for c in range(CHUNKS):
-            p_bank = ps.tile([P, GROUP, CHUNK], F32, name=f"p_bank{c}", tag=f"p{c}")
-            for a in range(PASSES):
-                grouped = sb.tile([P, CHUNK * PACK], BF16, name=f"grouped{c}_{a}", align_bytes=64)
-                dst = grouped[:].rearrange("p (m i j) -> p m j i", i=4, j=PACK)
-                src = w_raw[c, a][:].rearrange("p j (m i) -> p m j i", i=4)
-                if (c, a) in SCALAR_CASTS:
-                    nc.scalar.copy(dst, src)
-                else:
-                    nc.vector.tensor_copy(dst, src)
-                w_codes = sb.tile([P, CHUNK], U32, name=f"w_codes{c}_{a}", align_bytes=64)
-                w_scale = sb.tile([P, CHUNK], U8, name=f"w_scale{c}_{a}", align_bytes=64)
-                nc.vector.quantize_mx(out=w_codes[:].bitcast(FP8X4), scales=w_scale[:], in_=grouped[:])
-                for t in range(GROUP):
+        parts = {c: [(0, GROUP)] for c in range(CHUNKS - 1)}
+        parts[CHUNKS - 1] = [(0, GROUP // 2), (GROUP // 2, GROUP)]
+        p_banks = {
+            (c, lo): ps.tile([P, hi - lo, CHUNK], F32, name=f"p_bank{c}_{lo}", tag=f"p{c}_{lo}")
+            for c in range(CHUNKS)
+            for lo, hi in parts[c]
+        }
+        for c, a in ORDER:
+            if (c, a) == (0, 1):
+                x_codes.append(gather_words(1))
+            if (c, a) == ORDER[-1]:
+                grouped = linear[:, 0, :, :].rearrange("p c n -> p (c n)")[:, 64 : 64 + 256].bitcast(BF16)
+            else:
+                grouped = sb.tile([P, CHUNK * PACK], BF16, name=f"grouped{c}_{a}", align_bytes=64)[:]
+            dst = grouped.rearrange("p (m i j) -> p m j i", i=4, j=PACK)
+            src = w_raw[c, a].rearrange("p j (m i) -> p m j i", i=4)
+            if c < SCALAR_CHUNKS[a]:
+                nc.scalar.copy(dst, src)
+            else:
+                nc.vector.tensor_copy(dst, src)
+            w_codes = sb.tile([P, CHUNK], U32, name=f"w_codes{c}_{a}", align_bytes=64)
+            w_scale = sb.tile([P, CHUNK], U8, name=f"w_scale{c}_{a}", align_bytes=64)
+            nc.vector.quantize_mx(out=w_codes[:].bitcast(FP8X4), scales=w_scale[:], in_=grouped)
+            for lo, hi in parts[c]:
+                for t in range(lo, hi):
                     cols = slice(t * B, (t + 1) * B)
                     nc.tensor.matmul_mx(
-                        out=p_bank[:, t, :],
+                        out=p_banks[c, lo][:, t - lo, :],
                         lhsT=x_codes[a][:, cols].bitcast(FP8X4),
                         lhsT_scale=x_scale[4 * a : P, cols],
                         rhs=w_codes[:].bitcast(FP8X4),
                         rhs_scale=w_scale[:],
-                        start=(a == 0 and t == 0),
-                        stop=(a == PASSES - 1 and t == GROUP - 1),
+                        start=(a == 0 and t == lo),
+                        stop=(a == PASSES - 1 and t == hi - 1),
                     )
-            nc.scalar.activation(expo[:, c, :], p_bank[:].rearrange("p t n -> p (t n)"), ACT.Exp)
-            p_banks.append(p_bank)
+                if a == PASSES - 1:
+                    nc.scalar.activation(
+                        expo[:, c, lo * CHUNK : hi * CHUNK], p_banks[c, lo][:].rearrange("p t n -> p (t n)"), ACT.Exp
+                    )
 
+        def linear_part(c):
+            for lo, hi in parts[c]:
+                nc.vector.scalar_tensor_tensor(
+                    linear[:, lo:hi, c, :],
+                    p_banks[c, lo][:],
+                    X_CAP,
+                    gate[:, lo:hi].unsqueeze(2).to_broadcast([P, hi - lo, CHUNK]),
+                    ALU.max,
+                    ALU.mult,
+                )
+
+        for c in range(CHUNKS - 1):
+            linear_part(c)
         one_plus = sb.tile([P, CHUNKS, GROUP * CHUNK], F32, name="one_plus")
         nc.vector.tensor_scalar(one_plus[:], expo[:], EXP_CAP, 1.0, ALU.min, ALU.add)
+        linear_part(CHUNKS - 1)
 
-        linear = []
-        for c in range(CHUNKS):
-            lin = sb.tile([P, GROUP, CHUNK], F32, name=f"linear{c}")
-            nc.vector.scalar_tensor_tensor(
-                lin[:], p_banks[c][:], X_CAP, gate[:].unsqueeze(2).to_broadcast([P, GROUP, CHUNK]), ALU.max, ALU.mult
-            )
-            linear.append(lin)
+        stores = ((0, 2), (2, 3), (3, 4))
+        o_banks = [ps.tile([P, hi - lo, B], F32, name=f"o_bank{lo}", tag=f"o{lo}") for lo, hi in stores]
 
-        q_bank = ps.tile([P, N], F32, name="q_bank", tag="p0")
+        def pool(bank, lo, c, terms, start, stop):
+            for t in range(GROUP):
+                nc.tensor.matmul(
+                    bank[:, c - lo, :],
+                    terms(t),
+                    identity[:],
+                    start=(start and t == 0),
+                    stop=(stop and t == GROUP - 1),
+                    is_transpose=True,
+                )
+
+        for bank, (lo, hi) in zip(o_banks, stores):
+            for c in range(lo, hi):
+                pool(bank, lo, c, lambda t: linear[:, t, c, :], c == lo, False)
+
+        q_bank = ps.tile([P, N], F32, name="q_bank", tag="p0_0")
         nc.tensor.matmul_mx(
             out=q_bank[:],
             lhsT=cx_codes[:].bitcast(FP4X4),
@@ -156,29 +185,25 @@ def tile_list_expert_then_pool_kernel(tc, xq_words, xq_scales, wa, ga, cx_words,
             start=True,
             stop=True,
         )
-        context = sb.tile([P, N], F32, name="context")
-        nc.vector.tensor_scalar(context[:], q_bank[:], cap_sum[:], None, ALU.add)
 
-        o_banks = []
-        for c in range(CHUNKS):
-            o_bank = ps.tile([P, B], F32, name=f"o_bank{c}", tag=f"o{c}")
-            for t in range(GROUP):
-                nc.tensor.matmul(o_bank[:], linear[c][:, t, :], identity[:], start=(t == 0), stop=False, is_transpose=True)
-            o_banks.append(o_bank)
-        for c in range(CHUNKS):
-            nc.tensor.matmul(
-                o_banks[c][:], context[:, c * CHUNK : (c + 1) * CHUNK], identity[:], start=False, stop=False, is_transpose=True
-            )
-
-        for c in range(CHUNKS):
-            logs = sb.tile([P, GROUP, CHUNK], F32, name=f"logs{c}")
-            nc.scalar.activation(logs[:].rearrange("p t n -> p (t n)"), one_plus[:, c, :], ACT.Ln)
-            weighted = sb.tile([P, GROUP, CHUNK], F32, name=f"weighted{c}")
-            for t in range(GROUP):
-                nc.vector.tensor_scalar(weighted[:, t, :], logs[:, t, :], gate[:, t : t + 1], None, ALU.mult)
-                nc.tensor.matmul(
-                    o_banks[c][:], weighted[:, t, :], identity[:], start=False, stop=(t == GROUP - 1), is_transpose=True
-                )
-            result = sb.tile([P, B], F32, name=f"result{c}")
-            nc.vector.tensor_copy(result[:], o_banks[c][:])
-            nc.sync.dma_start(out=out[c * CHUNK : (c + 1) * CHUNK, :], in_=result[:])
+        for bank, (lo, hi) in zip(o_banks, stores):
+            for c in range(lo, hi):
+                logs = sb.tile([P, GROUP, CHUNK], F32, name=f"logs{c}")
+                flat = logs[:].rearrange("p t n -> p (t n)")
+                cuts = (0, GROUP * CHUNK) if c < CHUNKS - 1 else (0, (GROUP - 1) * CHUNK, GROUP * CHUNK)
+                for first, last in zip(cuts, cuts[1:]):
+                    nc.scalar.activation(flat[:, first:last], one_plus[:, c, first:last], ACT.Ln)
+                weighted = sb.tile([P, GROUP, CHUNK], F32, name=f"weighted{c}")
+                context = q_bank[:, c * CHUNK : (c + 1) * CHUNK]
+                nc.vector.scalar_tensor_tensor(weighted[:, 0, :], logs[:, 0, :], gate[:, 0:1], context, ALU.mult, ALU.add)
+                nc.vector.tensor_scalar(weighted[:, 1, :], logs[:, 1, :], gate[:, 1:2], cap_sum[:], ALU.mult, ALU.add)
+                for t in range(2, GROUP):
+                    nc.vector.tensor_scalar(weighted[:, t, :], logs[:, t, :], gate[:, t : t + 1], None, ALU.mult)
+                pool(bank, lo, c, lambda t: weighted[:, t, :], False, c == hi - 1)
+            result = sb.tile([P, hi - lo, B], F32, name=f"result{lo}")
+            if lo == 0:
+                nc.vector.tensor_copy(result[:], bank[:])
+            else:
+                nc.scalar.copy(result[:], bank[:])
+            rows = out[lo * CHUNK : hi * CHUNK, :].rearrange("(c p) b -> p c b", p=P)
+            nc.sync.dma_start(out=rows, in_=result[:])

import math
from contextlib import ExitStack

import concourse.mybir as mybir
from concourse.masks import make_identity

K, T, J, B, L, N = 1024, 2048, 512, 128, 512, 512
FLOPS = 2 * K * N * J + 2 * L * N * B

F32 = mybir.dt.float32
BF16 = mybir.dt.bfloat16
I32 = mybir.dt.int32
U32 = mybir.dt.uint32
U16 = mybir.dt.uint16
U8 = mybir.dt.uint8
FP8X4 = mybir.dt.float8_e4m3fn_x4
FP4X4 = mybir.dt.float4_e2m1fn_x4
ALU = mybir.AluOpType
ACT = mybir.ActivationFunctionType

P = 128
PACK = 4
K_PASS = P * PACK
PASSES = K // K_PASS
GROUP = J // B
CHUNK = 128
CHUNKS = N // CHUNK
EXP_CAP = 2.0**32
X_CAP = math.log(EXP_CAP)
W_LOADS = ((0, 0, 4), (1, 0, 1), (1, 1, 1), (1, 2, 1), (1, 3, 1))
ORDER = tuple((c, a) for a in range(PASSES) for c in range(CHUNKS))
SCALAR_CHUNKS = (3, 2)


def load_scale_rows(queue, plane, scales, passes):
    for quad in range(4):
        queue.dma_start(
            out=plane[32 * quad : 32 * quad + 4 * passes, :].bitcast(I32),
            in_=scales[:, 4 * quad : 4 * quad + 4, :].bitcast(I32),
        )


def tile_list_expert_then_pool_kernel(tc, xq_words, xq_scales, wa, ga, cx_words, cx_scales, wc_words, wc_scales, offs, out):
    nc = tc.nc
    with ExitStack() as ctx:
        sb = ctx.enter_context(tc.tile_pool(name="sb", bufs=1))
        ps = ctx.enter_context(tc.psum_pool(name="ps", bufs=1))

        offsets = sb.tile([P, J // 16], U16, name="offsets")
        nc.sync.dma_start(offsets[:], offs)

        x_plane = sb.tile([P, T], U8, name="x_plane", align_bytes=64)
        nc.gpsimd.memset(x_plane[:].bitcast(I32), 0)
        x_table = [sb.tile([P, T], U32, name=f"x_table{a}", align_bytes=64) for a in range(PASSES)]
        x_words = [xq_words[a].rearrange("p n t -> p (n t)").bitcast(I32) for a in range(PASSES)]
        nc.sync.dma_start(out=x_table[0][:].bitcast(I32), in_=x_words[0])
        load_scale_rows(nc.sync, x_plane, xq_scales, PASSES)
        gate = sb.tile([P, GROUP], F32, name="gate")
        nc.sync.dma_start(out=gate[:], in_=ga.rearrange("o (b t) -> (o b) t", t=GROUP))

        w_raw = {}
        for a, first, count in W_LOADS:
            raw = sb.tile([P, PACK, count * CHUNK], F32, name=f"w_raw{a}_{first}")
            rows = wa[a * K_PASS : (a + 1) * K_PASS, first * CHUNK : (first + count) * CHUNK]
            nc.sync.dma_start(out=raw[:], in_=rows.rearrange("(p j) n -> p j n", j=PACK))
            for c in range(count):
                w_raw[first + c, a] = raw[:, :, c * CHUNK : (c + 1) * CHUNK]
            if a == 0:
                nc.sync.dma_start(out=x_table[1][:].bitcast(I32), in_=x_words[1])

        wc_codes = sb.tile([P, N], U32, name="wc_codes", align_bytes=64)
        wc_plane = sb.tile([P, N], U8, name="wc_plane", align_bytes=64)
        cx_codes = sb.tile([P, 2 * B], U8, name="cx_codes", align_bytes=64)
        cx_plane = sb.tile([P, B], U8, name="cx_plane", align_bytes=64)
        nc.sync.dma_start(out=wc_codes[:].bitcast(I32), in_=wc_words[0].rearrange("p n t -> p (n t)").bitcast(I32))
        nc.sync.dma_start(out=cx_codes[:].bitcast(I32), in_=cx_words[0].bitcast(I32))
        identity = sb.tile([P, P], F32, name="identity")
        make_identity(nc, identity[:])
        nc.gpsimd.memset(wc_plane[:].bitcast(I32), 0)
        nc.gpsimd.memset(cx_plane[:].bitcast(I32), 0)
        load_scale_rows(nc.gpsimd, wc_plane, wc_scales, 1)
        load_scale_rows(nc.sync, cx_plane, cx_scales, 1)

        cap_terms = sb.tile([P, GROUP], F32, name="cap_terms")
        cap_sum = sb.tile([P, 1], F32, name="cap_sum")
        nc.scalar.activation(cap_terms[:], gate[:], ACT.Identity, scale=-X_CAP, accum_out=cap_sum[:])

        def gather_words(a):
            codes = sb.tile([P, J], U32, name=f"x_codes{a}", align_bytes=64)
            nc.vector.tensor_copy(codes[:].rearrange("p (t b) -> p b t", t=GROUP), x_table[a][:].indirect(offsets[:]))
            return codes

        x_codes = [gather_words(0)]
        picked_plane = sb.tile([P, J], U8, name="picked_plane", align_bytes=64)
        nc.vector.tensor_copy(picked_plane[:], x_plane[:].indirect(offsets[:]))
        x_scale = sb.tile([P, J], U8, name="x_scale", align_bytes=64)
        nc.vector.tensor_copy(
            x_scale[:].rearrange("p (t b) -> p t b", t=GROUP), picked_plane[:].rearrange("p (b t) -> p t b", t=GROUP)
        )

        linear = sb.tile([P, GROUP, CHUNKS, CHUNK], F32, name="linear", align_bytes=64)
        expo = sb.tile([P, CHUNKS, GROUP * CHUNK], F32, name="expo")
        parts = {c: [(0, GROUP)] for c in range(CHUNKS - 1)}
        parts[CHUNKS - 1] = [(0, GROUP // 2), (GROUP // 2, GROUP)]
        p_banks = {
            (c, lo): ps.tile([P, hi - lo, CHUNK], F32, name=f"p_bank{c}_{lo}", tag=f"p{c}_{lo}")
            for c in range(CHUNKS)
            for lo, hi in parts[c]
        }
        for c, a in ORDER:
            if (c, a) == (0, 1):
                x_codes.append(gather_words(1))
            if (c, a) == ORDER[-1]:
                grouped = linear[:, 0, :, :].rearrange("p c n -> p (c n)")[:, 64 : 64 + 256].bitcast(BF16)
            else:
                grouped = sb.tile([P, CHUNK * PACK], BF16, name=f"grouped{c}_{a}", align_bytes=64)[:]
            dst = grouped.rearrange("p (m i j) -> p m j i", i=4, j=PACK)
            src = w_raw[c, a].rearrange("p j (m i) -> p m j i", i=4)
            if c < SCALAR_CHUNKS[a]:
                nc.scalar.copy(dst, src)
            else:
                nc.vector.tensor_copy(dst, src)
            w_codes = sb.tile([P, CHUNK], U32, name=f"w_codes{c}_{a}", align_bytes=64)
            w_scale = sb.tile([P, CHUNK], U8, name=f"w_scale{c}_{a}", align_bytes=64)
            nc.vector.quantize_mx(out=w_codes[:].bitcast(FP8X4), scales=w_scale[:], in_=grouped)
            for lo, hi in parts[c]:
                for t in range(lo, hi):
                    cols = slice(t * B, (t + 1) * B)
                    nc.tensor.matmul_mx(
                        out=p_banks[c, lo][:, t - lo, :],
                        lhsT=x_codes[a][:, cols].bitcast(FP8X4),
                        lhsT_scale=x_scale[4 * a : P, cols],
                        rhs=w_codes[:].bitcast(FP8X4),
                        rhs_scale=w_scale[:],
                        start=(a == 0 and t == lo),
                        stop=(a == PASSES - 1 and t == hi - 1),
                    )
                if a == PASSES - 1:
                    nc.scalar.activation(
                        expo[:, c, lo * CHUNK : hi * CHUNK], p_banks[c, lo][:].rearrange("p t n -> p (t n)"), ACT.Exp
                    )

        def linear_part(c):
            for lo, hi in parts[c]:
                nc.vector.scalar_tensor_tensor(
                    linear[:, lo:hi, c, :],
                    p_banks[c, lo][:],
                    X_CAP,
                    gate[:, lo:hi].unsqueeze(2).to_broadcast([P, hi - lo, CHUNK]),
                    ALU.max,
                    ALU.mult,
                )

        for c in range(CHUNKS - 1):
            linear_part(c)
        one_plus = sb.tile([P, CHUNKS, GROUP * CHUNK], F32, name="one_plus")
        nc.vector.tensor_scalar(one_plus[:], expo[:], EXP_CAP, 1.0, ALU.min, ALU.add)
        linear_part(CHUNKS - 1)

        stores = ((0, 2), (2, 3), (3, 4))
        o_banks = [ps.tile([P, hi - lo, B], F32, name=f"o_bank{lo}", tag=f"o{lo}") for lo, hi in stores]

        def pool(bank, lo, c, terms, start, stop):
            for t in range(GROUP):
                nc.tensor.matmul(
                    bank[:, c - lo, :],
                    terms(t),
                    identity[:],
                    start=(start and t == 0),
                    stop=(stop and t == GROUP - 1),
                    is_transpose=True,
                )

        for bank, (lo, hi) in zip(o_banks, stores):
            for c in range(lo, hi):
                pool(bank, lo, c, lambda t: linear[:, t, c, :], c == lo, False)

        q_bank = ps.tile([P, N], F32, name="q_bank", tag="p0_0")
        nc.tensor.matmul_mx(
            out=q_bank[:],
            lhsT=cx_codes[:].bitcast(FP4X4),
            lhsT_scale=cx_plane[:],
            rhs=wc_codes[:].bitcast(FP8X4),
            rhs_scale=wc_plane[:],
            start=True,
            stop=True,
        )

        for bank, (lo, hi) in zip(o_banks, stores):
            for c in range(lo, hi):
                logs = sb.tile([P, GROUP, CHUNK], F32, name=f"logs{c}")
                flat = logs[:].rearrange("p t n -> p (t n)")
                cuts = (0, GROUP * CHUNK) if c < CHUNKS - 1 else (0, (GROUP - 1) * CHUNK, GROUP * CHUNK)
                for first, last in zip(cuts, cuts[1:]):
                    nc.scalar.activation(flat[:, first:last], one_plus[:, c, first:last], ACT.Ln)
                weighted = sb.tile([P, GROUP, CHUNK], F32, name=f"weighted{c}")
                context = q_bank[:, c * CHUNK : (c + 1) * CHUNK]
                nc.vector.scalar_tensor_tensor(weighted[:, 0, :], logs[:, 0, :], gate[:, 0:1], context, ALU.mult, ALU.add)
                nc.vector.tensor_scalar(weighted[:, 1, :], logs[:, 1, :], gate[:, 1:2], cap_sum[:], ALU.mult, ALU.add)
                for t in range(2, GROUP):
                    nc.vector.tensor_scalar(weighted[:, t, :], logs[:, t, :], gate[:, t : t + 1], None, ALU.mult)
                pool(bank, lo, c, lambda t: weighted[:, t, :], False, c == hi - 1)
            result = sb.tile([P, hi - lo, B], F32, name=f"result{lo}")
            if lo == 0:
                nc.vector.tensor_copy(result[:], bank[:])
            else:
                nc.scalar.copy(result[:], bank[:])
            rows = out[lo * CHUNK : hi * CHUNK, :].rearrange("(c p) b -> p c b", p=P)
            nc.sync.dma_start(out=rows, in_=result[:])
